import numpy as np
import ml_dtypes


def mxq(x, axis, fmt="e4m3"):
    dtype, down = {"e4m3": (ml_dtypes.float8_e4m3fn, 7), "e5m2": (ml_dtypes.float8_e5m2, 14)}[fmt]
    v = np.moveaxis(np.asarray(x, np.float32).astype(ml_dtypes.bfloat16).astype(np.float64), axis, -1)
    blocks = v.reshape(v.shape[:-1] + (-1, 32))
    amax = np.abs(blocks).max(-1, keepdims=True)
    byte = np.maximum(np.where(amax > 0, np.frexp(amax)[1] - 1 + 127, 0) - down, 1)
    scale = np.exp2(byte - 127.0)
    codes = (blocks / scale).astype(np.float32).astype(dtype).astype(np.float64)
    return np.moveaxis((codes * scale).reshape(v.shape), -1, axis)


WIDE = False


def mx_kscale(k):
    if not WIDE:
        return np.ones(k)
    levels = np.array([10, -10, 5, -5, 0])
    if k % 512:
        return np.exp2(np.random.permutation(np.resize(levels, k // 32))).repeat(32)
    a = np.empty((k // 512, 16))
    for p in range(k // 512):
        a[p, :8] = np.random.permutation(np.resize(levels, 8))
        for g in range(8):
            far = levels[np.abs(levels - a[p, g]) >= 10]
            a[p, g + 8] = far[np.random.randint(len(far))]
    return np.exp2(a.ravel()).repeat(32)


def f64(x):
    return np.asarray(x).astype(np.float64)


def striped(idx):
    return np.tile(idx.reshape(-1, 16).T, (8, 1)).astype(np.uint16)


def unstriped(offs):
    return offs[:16].T.reshape(-1).astype(np.int64)


E2M1 = np.array([0.0, 0.5, 1.0, 1.5, 2.0, 3.0, 4.0, 6.0, -0.0, -0.5, -1.0, -1.5, -2.0, -3.0, -4.0, -6.0])


def pack_weight(w, fmt):
    k, n = w.shape
    w = f64(np.asarray(w, np.float32).astype(ml_dtypes.bfloat16)).reshape(k // 32, 32, n)
    amax = np.abs(w).max(1)
    if fmt == "e4m3":
        byte = np.frexp(amax)[1] - 1 + 127 - 7
    else:
        mant, ex = np.frexp(amax / 6.0)
        byte = np.where(mant > 0.5, ex, ex - 1) + 127
    byte = np.clip(np.where(amax > 0, byte, 1), 1, 254)
    scaled = (w * np.exp2(127.0 - byte)[:, None, :]).reshape(k, n).astype(np.float32)
    by_word = np.ascontiguousarray(scaled.reshape(k // 512, 128, 4, n).transpose(0, 1, 3, 2))
    if fmt == "e4m3":
        words = by_word.astype(ml_dtypes.float8_e4m3fn).view(np.uint8)
    else:
        c = by_word.astype(ml_dtypes.float4_e2m1fn).view(np.uint8) & 0xF
        words = (c[..., 0::2] | (c[..., 1::2] << 4)).reshape(k // 512, 128, 2 * n)
    return np.ascontiguousarray(words), np.ascontiguousarray(byte.astype(np.uint8).reshape(k // 512, 16, n))


def unpack_weight(words, scales, fmt):
    g, _, n = scales.shape
    words = np.ascontiguousarray(words).reshape(g, 128, n, -1)
    if fmt == "e4m3":
        vals = words.view(ml_dtypes.float8_e4m3fn).astype(np.float64)
    else:
        nib = np.empty((g, 128, n, 4), np.uint8)
        nib[..., 0::2] = words & 0xF
        nib[..., 1::2] = words >> 4
        vals = E2M1[nib]
    vals = vals * np.repeat(np.exp2(scales.astype(np.float64) - 127.0), 8, axis=1)[..., None]
    return vals.transpose(0, 1, 3, 2).reshape(g * 512, n)


def gelu(v):
    return 0.5 * v * (1.0 + np.tanh(np.sqrt(2.0 / np.pi) * (v + 0.044715 * v**3)))


def often(T, S):
    return np.random.permutation(T)[(T * np.random.uniform(0, 1, S) ** 4).astype(np.int64)]


K, M, T, S, P, H, N = 1024, 512, 4096, 1024, 512, 1024, 384

def setup_inputs():
    n = np.random.standard_normal
    s, s2, u = mx_kscale(K)[:, None], mx_kscale(M)[:, None], mx_kscale(H)[:, None]
    d = {}
    d["tab_words"], d["tab_scales"] = pack_weight(n((K, T)) * s, "e4m3")
    d["tab2_words"], d["tab2_scales"] = pack_weight(n((M, T)) * s2, "e4m3")
    d["tab3_words"], d["tab3_scales"] = pack_weight(n((M, T)) * s2, "e4m3")
    d["offs"] = striped(np.random.permutation(T)[:S])
    d["offs2"] = striped(np.random.permutation(T)[:S])
    d["offs3"] = striped(np.random.permutation(T)[:S])
    d["pos1"] = striped(np.random.permutation(S)[:P])
    d["pos2"] = striped(often(S, P))
    d["pos3"] = striped(often(S, P))
    d["w1"] = (0.8 * n((K, H)) / K ** 0.5 / s).astype(np.float32)
    d["w2_words"], d["w2_scales"] = pack_weight(0.8 * n((M, H)) / M ** 0.5 / s2, "e2m1")
    d["w3_words"], d["w3_scales"] = pack_weight(2.4 * n((M, H)) / M ** 0.5 / s2, "e4m3")
    d["gain"] = (0.5 * np.exp(0.3 * n(H)) * u[:, 0]).astype(np.float32)
    d["w4"] = (1.8 * n((H, N)) / H ** 0.5 / u).astype(np.float32)
    d["w5_words"], d["w5_scales"] = pack_weight(n((H, N)) / H ** 0.5 / u, "e2m1")
    return d

def reference(tab_words, tab_scales, tab2_words, tab2_scales, tab3_words, tab3_scales, offs, offs2, offs3,
              pos1, pos2, pos3, w1, w2_words, w2_scales, w3_words, w3_scales, gain, w4, w5_words, w5_scales):
    v = unpack_weight(tab_words, tab_scales, "e4m3")[:, unstriped(offs)]
    v2 = unpack_weight(tab2_words, tab2_scales, "e4m3")[:, unstriped(offs2)]
    v3 = unpack_weight(tab3_words, tab3_scales, "e4m3")[:, unstriped(offs3)]
    a = mxq(f64(w1), 0, "e4m3").T @ v
    b = unpack_weight(w2_words, w2_scales, "e2m1").T @ v2
    d = unpack_weight(w3_words, w3_scales, "e4m3").T @ v3
    mis = np.square(a[:, unstriped(pos1)] - b[:, unstriped(pos2)])
    gate = 1.0 / (1.0 + np.exp(-d[:, unstriped(pos3)]))
    z = mxq(f64(gain)[:, None] * mis * gate, 0, "e4m3")
    y = np.tanh(mxq(f64(w4), 0, "e4m3").T @ z)
    return y + (unpack_weight(w5_words, w5_scales, "e2m1").T @ z)

@@ -1,0 +1,247 @@
+from contextlib import ExitStack
+
+import concourse.mybir as mybir
+
+F32 = mybir.dt.float32
+BF16 = mybir.dt.bfloat16
+I32 = mybir.dt.int32
+U32 = mybir.dt.uint32
+U16 = mybir.dt.uint16
+U8 = mybir.dt.uint8
+FP8X4 = mybir.dt.float8_e4m3fn_x4
+FP4X4 = mybir.dt.float4_e2m1fn_x4
+ACT = mybir.ActivationFunctionType
+ALU = mybir.AluOpType
+
+FLOPS = 5100273664
+
+P = 128
+T = 4096
+S = 1024
+J = 512
+H = 1024
+N = 384
+KP = 512
+PLANE_V2, PLANE_V3, PLANE_V = 0, 4, 8
+PLANE_W2, PLANE_W3 = 0, 4
+RAW = 32
+LAST_CHUNKS = ((0, 256), (256, 384), (384, 512))
+
+
+def tile_list_laundry_batch_scores_kernel(
+    tc, tab_words, tab_scales, tab2_words, tab2_scales, tab3_words, tab3_scales, offs, offs2, offs3,
+    pos1, pos2, pos3, w1, w2_words, w2_scales, w3_words, w3_scales, gain, w4, w5_words, w5_scales, out,
+):
+    nc = tc.nc
+    with ExitStack() as ctx:
+        keep = ctx.enter_context(tc.tile_pool(name="keep", bufs=1))
+        ring = ctx.enter_context(tc.tile_pool(name="ring", bufs=3))
+        shared = ctx.enter_context(tc.tile_pool(name="shared", bufs=1))
+        psum = ctx.enter_context(tc.psum_pool(name="psum", bufs=8))
+
+        def load_list(src, name):
+            t = keep.tile(list(src.shape), U16, name=name)
+            nc.sync.dma_start(t[:], src)
+            return t
+
+        def zeroed(t, eng):
+            eng.memset(t[:].bitcast(I32), 0)
+            return t
+
+        def placed(shape, dtype, name, kib):
+            return shared.tile(shape, dtype, name=name, offset=1024 * kib, align_bytes=64)
+
+        def load_scale_rows(eng, plane, first_row, scales):
+            rows = 4 * scales.shape[0]
+            for q in range(4):
+                p0 = 32 * q + first_row
+                eng[q].dma_start(plane[p0:p0 + rows, :].bitcast(I32), scales[:, 4 * q:4 * q + 4, :].bitcast(I32))
+
+        def load_table_words(words, a, name, kib):
+            t = placed([P, T], I32, name, kib)
+            nc.sync.dma_start(t[:], words[a].rearrange("p t i -> p (t i)").bitcast(I32))
+            return t
+
+        def gather_words(table, lst, name):
+            g = keep.tile([P, S], U32, name=name, align_bytes=64)
+            nc.vector.tensor_copy(g[:], table[:].bitcast(U32).indirect(lst[:]))
+            return g
+
+        def gather_scales(plane, lst, name):
+            g = keep.tile([P, S], U8, name=name, align_bytes=64)
+            nc.vector.tensor_copy(g[:], plane[:].indirect(lst[:]))
+            return g
+
+        def first_stage(passes):
+            row = ring.tile([P, S], F32, name="row", tag="row", bufs=8)
+            for h in range(S // 512):
+                cols = slice(512 * h, 512 * (h + 1))
+                acc = psum.tile([P, 512], F32, name="acc", tag="bank")
+                for i, (wc, ws, vc, vs, k) in enumerate(passes):
+                    nc.tensor.matmul_mx(out=acc[:], lhsT=wc, lhsT_scale=ws, rhs=vc[:, cols].bitcast(FP8X4),
+                                        rhs_scale=vs[k:P, cols], start=(i == 0), stop=(i == len(passes) - 1))
+                nc.scalar.copy(row[:, cols], acc[:])
+            return row
+
+        def load_w1(a, b):
+            raw = placed([P, 4, 512], F32, "w1raw%d%d" % (a, b), RAW + 8 * (a + 2 * b))
+            nc.sync.dma_start(raw[:], w1[KP * a:KP * (a + 1), 512 * b:512 * (b + 1)].rearrange("(p j) c -> p j c", j=4))
+            return raw
+
+        def cast(dst, src):
+            nc.scalar.copy(dst, src)
+
+        def quantise_w1(raw, a, b):
+            bf = ring.tile([P, 2048], BF16, name="bf", tag="bf", bufs=2, align_bytes=64)
+            cast(bf[:].rearrange("p (t m j) -> p m j t", t=4, j=4), raw[:].rearrange("p j (m t) -> p m j t", t=4))
+            codes = keep.tile([P, 512], U32, name="w1c%d%d" % (a, b), align_bytes=64)
+            scales = keep.tile([P, 512], U8, name="w1s%d%d" % (a, b), align_bytes=64)
+            nc.vector.quantize_mx(out=codes[:].bitcast(FP8X4), scales=scales[:], in_=bf[:])
+            return codes, scales
+
+        w3_plane = zeroed(placed([P, H], U8, "w3_plane", RAW + 8), nc.gpsimd)
+        v3_plane = zeroed(placed([P, T], U8, "v3_plane", 0), nc.vector)
+        w2_plane = zeroed(placed([P, H], U8, "w2_plane", RAW + 24), nc.gpsimd)
+        w5s = zeroed(keep.tile([P, 2 * N], U8, name="w5s", align_bytes=64), nc.gpsimd)
+        idx3 = load_list(offs3, "idx3")
+        idx = load_list(offs, "idx")
+        idx2 = load_list(offs2, "idx2")
+        p3 = load_list(pos3, "p3")
+        p2 = load_list(pos2, "p2")
+        p1 = load_list(pos1, "p1")
+        w3_raw = placed([P, H], I32, "w3_raw", RAW)
+        nc.sync.dma_start(w3_raw[:], w3_words[0].rearrange("p c i -> p (c i)").bitcast(I32))
+        table3 = load_table_words(tab3_words, 0, "table3", 16)
+        load_scale_rows([nc.scalar] * 4, v3_plane, PLANE_V3, tab3_scales)
+        load_scale_rows([nc.gpsimd] + [nc.scalar] * 3, w3_plane, 0, w3_scales)
+        w2_raw = placed([P, 2 * H], U8, "w2_raw", RAW + 16)
+        nc.gpsimd.dma_start(w2_raw[:].bitcast(I32), w2_words[0].bitcast(I32))
+        load_scale_rows([nc.gpsimd] * 4, w2_plane, 0, w2_scales)
+        gain_t = keep.tile([P, 2, 4], F32, name="gain_t")
+        nc.gpsimd.dma_start(gain_t[:], gain.rearrange("(b p t) -> p b t", b=2, t=4))
+        w5c = keep.tile([P, 2, 2 * N], U8, name="w5c", align_bytes=64)
+        nc.gpsimd.dma_start(w5c[:].bitcast(I32), w5_words.rearrange("a p c -> p a c").bitcast(I32))
+        for q in range(4):
+            nc.gpsimd.dma_start(w5s[32 * q:32 * q + 4, :].rearrange("r (a n) -> r a n", a=2).bitcast(I32),
+                                w5_scales[:, 4 * q:4 * q + 4, :].rearrange("a r n -> r a n").bitcast(I32))
+
+        def deal(src, dtype, name):
+            dst = keep.tile(list(src.shape), src.dtype, name=name, align_bytes=64)
+            nc.vector.tensor_copy(dst[:].bitcast(dtype).rearrange("p (b t m) -> p b t m", b=2, t=4),
+                                  src[:].bitcast(dtype).rearrange("p (b m t) -> p b t m", b=2, t=4))
+            return dst
+
+        v3s = gather_scales(v3_plane, idx3, "v3s")
+        table2 = load_table_words(tab2_words, 0, "table2", 0)
+        w3c = keep.tile([P, H], I32, name="w3c", align_bytes=64)
+        nc.vector.tensor_copy(w3c[:].rearrange("p (b t m) -> p b m t", b=2, t=4), w3_raw[:].rearrange("p (b m t) -> p b m t", b=2, t=4))
+        w3s = deal(w3_plane, U8, "w3s")
+        v3c = gather_words(table3, idx3, "v3c")
+        v2_plane = zeroed(placed([P, T], U8, "v2_plane", 16), nc.vector)
+        v_plane = zeroed(placed([P, T], U8, "v_plane", 20), nc.vector)
+        load_scale_rows([nc.sync] * 4, v2_plane, PLANE_V2, tab2_scales)
+        load_scale_rows([nc.sync] * 4, v_plane, PLANE_V, tab_scales)
+        w2c = deal(w2_raw, U16, "w2c")
+        w2s = deal(w2_plane, U8, "w2s")
+        w1_raw = {}
+        for b in range(2):
+            for a in range(2):
+                w1_raw[a, b] = load_w1(a, b)
+        v2s = gather_scales(v2_plane, idx2, "v2s")
+        v2c = gather_words(table2, idx2, "v2c")
+        vs = gather_scales(v_plane, idx, "vs")
+        table_a0 = load_table_words(tab_words, 0, "table_a0", 16)
+        table_a1 = load_table_words(tab_words, 1, "table_a1", 0)
+
+        gate = [keep.tile([P, 4, J], F32, name="gate%d" % b) for b in range(2)]
+        for c in range(8):
+            b, t = divmod(c, 4)
+            cols = slice(P * c, P * (c + 1))
+            d_row = first_stage([(w3c[:, cols].bitcast(FP8X4), w3s[:, cols], v3c, v3s, PLANE_V3)])
+            nc.vector.tensor_copy(gate[b][:, t, :], d_row[:].indirect(p3[:]))
+
+        def finish_gate(b):
+            nc.scalar.activation(gate[b][:], gate[b][:], ACT.Sigmoid)
+            for t in range(4):
+                nc.scalar.mul(gate[b][:, t, :], gate[b][:, t, :], gain_t[:, b, t:t + 1])
+
+        vc = [gather_words(table_a0, idx, "vc0"), gather_words(table_a1, idx, "vc1")]
+        w1q = {}
+
+        picked_b = [keep.tile([P, 4, J], F32, name="picked_b%d" % b) for b in range(2)]
+        for c in range(8):
+            b, t = divmod(c, 4)
+            cols = slice(P * c, P * (c + 1))
+            b_row = first_stage([(w2c[:, 2 * P * c:2 * P * (c + 1)].bitcast(FP4X4), w2s[:, cols], v2c, v2s, PLANE_V2)])
+            nc.vector.tensor_copy(picked_b[b][:, t, :], b_row[:].indirect(p2[:]))
+            if c in (3, 5):
+                a = len(w1q)
+                w1q[a, 0] = quantise_w1(w1_raw[a, 0], a, 0)
+
+        def make_z(b, a_rows, lo, hi):
+            w = hi - lo
+            sq = keep.tile([P, 4, w], F32, name="sq%d_%d" % (b, lo))
+            for t in range(4):
+                nc.vector.tensor_tensor(sq[:, t, :], a_rows[t][:].indirect(p1[:, lo // 16:hi // 16]),
+                                        picked_b[b][:, t, lo:hi], ALU.subtract)
+                nc.scalar.activation(sq[:, t, :], sq[:, t, :], ACT.Square)
+            zbf = keep.tile([P, 4 * w], BF16, name="zbf%d_%d" % (b, lo), align_bytes=64)
+            nc.vector.tensor_tensor(zbf[:].rearrange("p (c i t) -> p c t i", i=4, t=4),
+                                    sq[:].rearrange("p t (c i) -> p c t i", i=4),
+                                    gate[b][:, :, lo:hi].rearrange("p t (c i) -> p c t i", i=4), ALU.mult)
+            zc = keep.tile([P, w], U32, name="zc%d_%d" % (b, lo), align_bytes=64)
+            zs = keep.tile([P, w], U8, name="zs%d_%d" % (b, lo), align_bytes=64)
+            nc.vector.quantize_mx(out=zc[:].bitcast(FP8X4), scales=zs[:], in_=zbf[:])
+            return zc, zs
+
+        def a_rows_of(b):
+            rows = []
+            for t in range(4):
+                cols = slice(P * t, P * (t + 1))
+                rows.append(first_stage([
+                    (w1q[a, b][0][:, cols].bitcast(FP8X4), w1q[a, b][1][:, cols], vc[a], vs, PLANE_V + 4 * a)
+                    for a in range(2)]))
+            return rows
+
+        rows0 = a_rows_of(0)
+        for a in range(2):
+            w1q[a, 1] = quantise_w1(w1_raw[a, 1], a, 1)
+        finish_gate(0)
+        rows1 = a_rows_of(1)
+        z0 = make_z(0, rows0, 0, J)
+        finish_gate(1)
+        w4c = keep.tile([P, 2 * N], U32, name="w4c", align_bytes=64)
+        w4s = keep.tile([P, 2 * N], U8, name="w4s", align_bytes=64)
+        for a in range(2):
+            raw = placed([P, 4, N], F32, "w4raw%d" % a, RAW + 8 * a)
+            nc.sync.dma_start(raw[:], w4[KP * a:KP * (a + 1), :].rearrange("(p j) n -> p j n", j=4))
+            w4bf = ring.tile([P, 4 * N], BF16, name="w4bf", tag="bf", bufs=2, align_bytes=64)
+            cast(w4bf[:].rearrange("p (c i j) -> p c j i", i=4, j=4), raw[:].rearrange("p j (c i) -> p c j i", i=4))
+            for lo, hi in ((0, 256), (256, N)):
+                nc.vector.quantize_mx(out=w4c[:, N * a + lo:N * a + hi].bitcast(FP8X4), scales=w4s[:, N * a + lo:N * a + hi],
+                                      in_=w4bf[:, 4 * lo:4 * hi])
+
+        out_v = out.rearrange("(i p) j -> p i j", p=P)
+        for lo, hi in LAST_CHUNKS:
+            z1 = make_z(1, rows1, lo, hi)
+            for j0 in range(lo, hi, P):
+                zp = [(z0[0][:, j0:j0 + P], z0[1][:, j0:j0 + P]),
+                      (z1[0][:, j0 - lo:j0 - lo + P], z1[1][:, j0 - lo:j0 - lo + P])]
+                y4 = psum.tile([P, 3, P], F32, name="y4", tag="bank")
+                y5 = psum.tile([P, 3, P], F32, name="y5", tag="bank")
+                for i in range(3):
+                    for b in range(2):
+                        n0 = N * b + P * i
+                        nc.tensor.matmul_mx(out=y4[:, i, :], lhsT=w4c[:, n0:n0 + P].bitcast(FP8X4), lhsT_scale=w4s[:, n0:n0 + P],
+                                            rhs=zp[b][0].bitcast(FP8X4), rhs_scale=zp[b][1], start=(b == 0), stop=(b == 1))
+                for i in range(3):
+                    for b in range(2):
+                        n0 = N * b + P * i
+                        nc.tensor.matmul_mx(out=y5[:, i, :], lhsT=w5c[:, b, 2 * P * i:2 * P * (i + 1)].bitcast(FP4X4),
+                                            lhsT_scale=w5s[:, n0:n0 + P],
+                                            rhs=zp[b][0].bitcast(FP8X4), rhs_scale=zp[b][1], start=(b == 0), stop=(b == 1))
+                bounded = ring.tile([P, 3, P], F32, name="bounded", tag="bounded", bufs=2)
+                nc.scalar.activation(bounded[:], y4[:], ACT.Tanh)
+                res = ring.tile([P, 3, P], F32, name="res", tag="res", bufs=3)
+                nc.vector.tensor_tensor(res[:], y5[:], bounded[:], ALU.add)
+                nc.sync.dma_start(out_v[:, :, j0:j0 + P], res[:])

@@ -24,8 +24,22 @@ N = 384
 KP = 512
 PLANE_V2, PLANE_V3, PLANE_V = 0, 4, 8
 PLANE_W2, PLANE_W3 = 0, 4
-RAW = 32
-LAST_CHUNKS = ((0, 256), (256, 384), (384, 512))
+V3C = 0
+V3 = V3C + 4096 - 64
+W1_AT = (V3 + 4096 - 64, V3 + 4096 - 64 + 8192)
+A1 = W1_AT[1] + 8192
+T2 = A1 + 16384 - 64
+T3 = T2 + 16384 - 64
+V2S = T3 + 16384 - 64
+W4R = V2S + 1024 - 64
+V2 = W4R + 12288
+D0 = V2 + 4096 - 64
+VP = D0 + 2048 - 64
+A0 = VP + 64
+ROWS = A0 + 16384
+PAD = (4096, 0, 4096, 4096, 0, 0, 0, 0)
+SLOT = [ROWS + sum(PAD[:i + 1]) + 4160 * i for i in range(8)]
+LAST_CHUNKS = ((0, 384), (384, 512))
 
 
 def tile_list_laundry_batch_scores_kernel(
@@ -49,7 +63,7 @@ def tile_list_laundry_batch_scores_kernel(
             return t
 
         def placed(shape, dtype, name, kib):
-            return shared.tile(shape, dtype, name=name, offset=1024 * kib, align_bytes=64)
+            return shared.tile(shape, dtype, name=name, offset=kib, align_bytes=64)
 
         def load_scale_rows(eng, plane, first_row, scales):
             rows = 4 * scales.shape[0]
@@ -62,18 +76,16 @@ def tile_list_laundry_batch_scores_kernel(
             nc.sync.dma_start(t[:], words[a].rearrange("p t i -> p (t i)").bitcast(I32))
             return t
 
-        def gather_words(table, lst, name):
-            g = keep.tile([P, S], U32, name=name, align_bytes=64)
+        def gather_words(table, lst, g):
             nc.vector.tensor_copy(g[:], table[:].bitcast(U32).indirect(lst[:]))
             return g
 
-        def gather_scales(plane, lst, name):
-            g = keep.tile([P, S], U8, name=name, align_bytes=64)
+        def gather_scales(plane, lst, g):
             nc.vector.tensor_copy(g[:], plane[:].indirect(lst[:]))
             return g
 
-        def first_stage(passes):
-            row = ring.tile([P, S], F32, name="row", tag="row", bufs=8)
+        def first_stage(passes, name, at):
+            row = placed([P, S], F32, name, at)
             for h in range(S // 512):
                 cols = slice(512 * h, 512 * (h + 1))
                 acc = psum.tile([P, 512], F32, name="acc", tag="bank")
@@ -84,9 +96,24 @@ def tile_list_laundry_batch_scores_kernel(
             return row
 
         def load_w1(a, b):
-            raw = placed([P, 4, 512], F32, "w1raw%d%d" % (a, b), RAW + 8 * (a + 2 * b))
+            raw = placed([P, 4, 512], F32, "w1raw%d%d" % (a, b), W1_AT[a])
             nc.sync.dma_start(raw[:], w1[KP * a:KP * (a + 1), 512 * b:512 * (b + 1)].rearrange("(p j) c -> p j c", j=4))
             return raw
+
+        def load_w4(a, raw):
+            nc.sync.dma_start(raw[:], w4[KP * a:KP * (a + 1), :].rearrange("(p j) n -> p j n", j=4))
+            return raw
+
+        w4c = keep.tile([P, 2 * N], U32, name="w4c", align_bytes=64)
+        w4s = keep.tile([P, 2 * N], U8, name="w4s", align_bytes=64)
+
+        def quantise_w4(a, cast):
+            raw = w4_raw[:, a]
+            w4bf = placed([P, 4 * N], BF16, "w4bf%d" % a, SLOT[2 + a] + 64)
+            cast(w4bf[:].rearrange("p (c i j) -> p c j i", i=4, j=4), raw.rearrange("p j (c i) -> p c j i", i=4))
+            for lo, hi in ((0, 256), (256, N)):
+                nc.vector.quantize_mx(out=w4c[:, N * a + lo:N * a + hi].bitcast(FP8X4), scales=w4s[:, N * a + lo:N * a + hi],
+                                      in_=w4bf[:, 4 * lo:4 * hi])
 
         def cast(dst, src):
             nc.scalar.copy(dst, src)
@@ -94,136 +121,186 @@ def tile_list_laundry_batch_scores_kernel(
         def quantise_w1(raw, a, b):
             bf = ring.tile([P, 2048], BF16, name="bf", tag="bf", bufs=2, align_bytes=64)
             cast(bf[:].rearrange("p (t m j) -> p m j t", t=4, j=4), raw[:].rearrange("p j (m t) -> p m j t", t=4))
-            codes = keep.tile([P, 512], U32, name="w1c%d%d" % (a, b), align_bytes=64)
-            scales = keep.tile([P, 512], U8, name="w1s%d%d" % (a, b), align_bytes=64)
+            at = (T2 + 64 + 3072 + 8192, A1 + 10240)[b] + 2560 * a
+            codes = placed([P, 512], U32, "w1c%d%d" % (a, b), at)
+            scales = placed([P, 512], U8, "w1s%d%d" % (a, b), at + 2048)
             nc.vector.quantize_mx(out=codes[:].bitcast(FP8X4), scales=scales[:], in_=bf[:])
             return codes, scales
 
-        w3_plane = zeroed(placed([P, H], U8, "w3_plane", RAW + 8), nc.gpsimd)
-        v3_plane = zeroed(placed([P, T], U8, "v3_plane", 0), nc.vector)
-        w2_plane = zeroed(placed([P, H], U8, "w2_plane", RAW + 24), nc.gpsimd)
-        w5s = zeroed(keep.tile([P, 2 * N], U8, name="w5s", align_bytes=64), nc.gpsimd)
+        clock = keep.tile([P, 32], F32, name="clock")
+
+        def probe(i, ap):
+            if i in ():
+                nc.gpsimd.tensor_copy(clock[:, i:i + 1], ap)
+
+        v3_plane = zeroed(placed([P, T], U8, "v3_plane", V3), nc.vector)
+        w3_plane = zeroed(keep.tile([P, H], U8, name="w3_plane", align_bytes=64), nc.gpsimd)
+        v2_plane = zeroed(placed([P, T], U8, "v2_plane", V2), nc.vector)
+        v_plane = zeroed(placed([P, T], U8, "v_plane", VP), nc.vector)
+        w2_plane = zeroed(keep.tile([P, H], U8, name="w2_plane", align_bytes=64), nc.vector)
+        warm = keep.tile([P, 8], F32, name="warm")
+        nc.vector.memset(warm[:], 0.0)
+        nc.scalar.activation(warm[:, 1:2], warm[:, 0:1], ACT.Sigmoid)
         idx3 = load_list(offs3, "idx3")
         idx = load_list(offs, "idx")
         idx2 = load_list(offs2, "idx2")
         p3 = load_list(pos3, "p3")
         p2 = load_list(pos2, "p2")
         p1 = load_list(pos1, "p1")
-        w3_raw = placed([P, H], I32, "w3_raw", RAW)
+        w3_raw = placed([P, H], I32, "w3_raw", W1_AT[1])
         nc.sync.dma_start(w3_raw[:], w3_words[0].rearrange("p c i -> p (c i)").bitcast(I32))
-        table3 = load_table_words(tab3_words, 0, "table3", 16)
-        load_scale_rows([nc.scalar] * 4, v3_plane, PLANE_V3, tab3_scales)
-        load_scale_rows([nc.gpsimd] + [nc.scalar] * 3, w3_plane, 0, w3_scales)
-        w2_raw = placed([P, 2 * H], U8, "w2_raw", RAW + 16)
-        nc.gpsimd.dma_start(w2_raw[:].bitcast(I32), w2_words[0].bitcast(I32))
-        load_scale_rows([nc.gpsimd] * 4, w2_plane, 0, w2_scales)
-        gain_t = keep.tile([P, 2, 4], F32, name="gain_t")
-        nc.gpsimd.dma_start(gain_t[:], gain.rearrange("(b p t) -> p b t", b=2, t=4))
-        w5c = keep.tile([P, 2, 2 * N], U8, name="w5c", align_bytes=64)
-        nc.gpsimd.dma_start(w5c[:].bitcast(I32), w5_words.rearrange("a p c -> p a c").bitcast(I32))
-        for q in range(4):
-            nc.gpsimd.dma_start(w5s[32 * q:32 * q + 4, :].rearrange("r (a n) -> r a n", a=2).bitcast(I32),
-                                w5_scales[:, 4 * q:4 * q + 4, :].rearrange("a r n -> r a n").bitcast(I32))
+        table3 = load_table_words(tab3_words, 0, "table3", T3)
+        w4_raw = {}
 
-        def deal(src, dtype, name):
-            dst = keep.tile(list(src.shape), src.dtype, name=name, align_bytes=64)
+        load_scale_rows([nc.scalar] * 4, v3_plane, PLANE_V3, tab3_scales)
+        load_scale_rows([nc.gpsimd] * 2 + [nc.scalar] * (4 - 2), w3_plane, 0, w3_scales)
+        load_scale_rows([nc.gpsimd] * 4, v2_plane, PLANE_V2, tab2_scales)
+        load_scale_rows([nc.sync] * 4, v_plane, PLANE_V, tab_scales)
+        load_scale_rows([nc.sync] * 4, w2_plane, 0, w2_scales)
+
+        def deal(src, dtype, dst):
             nc.vector.tensor_copy(dst[:].bitcast(dtype).rearrange("p (b t m) -> p b t m", b=2, t=4),
                                   src[:].bitcast(dtype).rearrange("p (b m t) -> p b t m", b=2, t=4))
             return dst
 
-        v3s = gather_scales(v3_plane, idx3, "v3s")
-        table2 = load_table_words(tab2_words, 0, "table2", 0)
         w3c = keep.tile([P, H], I32, name="w3c", align_bytes=64)
         nc.vector.tensor_copy(w3c[:].rearrange("p (b t m) -> p b m t", b=2, t=4), w3_raw[:].rearrange("p (b m t) -> p b m t", b=2, t=4))
-        w3s = deal(w3_plane, U8, "w3s")
-        v3c = gather_words(table3, idx3, "v3c")
-        v2_plane = zeroed(placed([P, T], U8, "v2_plane", 16), nc.vector)
-        v_plane = zeroed(placed([P, T], U8, "v_plane", 20), nc.vector)
-        load_scale_rows([nc.sync] * 4, v2_plane, PLANE_V2, tab2_scales)
-        load_scale_rows([nc.sync] * 4, v_plane, PLANE_V, tab_scales)
-        w2c = deal(w2_raw, U16, "w2c")
-        w2s = deal(w2_plane, U8, "w2s")
         w1_raw = {}
-        for b in range(2):
-            for a in range(2):
-                w1_raw[a, b] = load_w1(a, b)
-        v2s = gather_scales(v2_plane, idx2, "v2s")
-        v2c = gather_words(table2, idx2, "v2c")
-        vs = gather_scales(v_plane, idx, "vs")
-        table_a0 = load_table_words(tab_words, 0, "table_a0", 16)
-        table_a1 = load_table_words(tab_words, 1, "table_a1", 0)
+        w1_raw[1, 0] = load_w1(1, 0)
+        v3s = gather_scales(v3_plane, idx3, keep.tile([P, S], U8, name="v3s", align_bytes=64))
+        w1_raw[0, 0] = load_w1(0, 0)
+        w3s = deal(w3_plane, U8, keep.tile([P, H], U8, name="w3s", align_bytes=64))
+        v3c = placed([P, S], U32, "v3c", V3C)
+        for h in range(2):
+            nc.vector.tensor_copy(v3c[:, 512 * h:512 * (h + 1)], table3[:].bitcast(U32).indirect(idx3[:, 32 * h:32 * (h + 1)]))
+        table2 = load_table_words(tab2_words, 0, "table2", T2)
+        w2_raw = placed([P, 2 * H], U8, "w2_raw", T3 + 64)
+        nc.sync.dma_start(w2_raw[:].bitcast(I32), w2_words[0].bitcast(I32))
+        v2s = gather_scales(v2_plane, idx2, placed([P, S], U8, "v2s", V2S))
+        vs = gather_scales(v_plane, idx, placed([P, S], U8, "vs", T3 + 4096))
+        table_a0 = load_table_words(tab_words, 0, "table_a0", A0)
+        gain_t = placed([P, 2, 4], F32, "gain_t", T3 + 5120)
+        nc.sync.dma_start(gain_t[:], gain.rearrange("(b p t) -> p b t", b=2, t=4))
+        w5c = placed([P, 2, 2 * N], U8, "w5c", T3 + 5184)
+        nc.sync.dma_start(w5c[:].bitcast(I32), w5_words.rearrange("a p c -> p a c").bitcast(I32))
+        w5s = zeroed(placed([P, 2 * N], U8, "w5s", T3 + 6720), nc.vector)
+        for q in range(4):
+            nc.sync.dma_start(w5s[32 * q:32 * q + 4, :].rearrange("r (a n) -> r a n", a=2).bitcast(I32),
+                              w5_scales[:, 4 * q:4 * q + 4, :].rearrange("a r n -> r a n").bitcast(I32))
 
-        gate = [keep.tile([P, 4, J], F32, name="gate%d" % b) for b in range(2)]
+        picked_d = []
         for c in range(8):
+            if c == 4:
+                v2c = gather_words(table2, idx2, placed([P, S], U32, "v2c", SLOT[3] + 64 - 4096))
+                table_a1 = load_table_words(tab_words, 1, "table_a1", A1)
+                w2c = deal(w2_raw, U16, placed([P, 2 * H], U8, "w2c", T2 + 64))
+                w2s = deal(w2_plane, U8, placed([P, H], U8, "w2s", T2 + 64 + 2048))
             b, t = divmod(c, 4)
             cols = slice(P * c, P * (c + 1))
-            d_row = first_stage([(w3c[:, cols].bitcast(FP8X4), w3s[:, cols], v3c, v3s, PLANE_V3)])
-            nc.vector.tensor_copy(gate[b][:, t, :], d_row[:].indirect(p3[:]))
+            d_row = first_stage([(w3c[:, cols].bitcast(FP8X4), w3s[:, cols], v3c, v3s, PLANE_V3)], "d%d" % c, SLOT[c])
+            if c in (0, 4, 5, 6, 7):
+                picked_d.append(placed([P, J], F32, "picked_d%d" % c, D0 if c == 0 else T2 + 64 + 3072 + 2048 * (c - 4)))
+            else:
+                picked_d.append(keep.tile([P, J], F32, name="picked_d%d" % c))
+            nc.vector.tensor_copy(picked_d[c][:], d_row[:].indirect(p3[:]))
+            probe(c, picked_d[c][:, 0:1])
 
-        def finish_gate(b):
-            nc.scalar.activation(gate[b][:], gate[b][:], ACT.Sigmoid)
-            for t in range(4):
-                nc.scalar.mul(gate[b][:, t, :], gate[b][:, t, :], gain_t[:, b, t:t + 1])
+        def finish_gate(c, dst):
+            b, t = divmod(c, 4)
+            nc.scalar.activation(dst[:, t, :], picked_d[c][:], ACT.Sigmoid)
+            if c in (4, 5, 6, 7):
+                nc.vector.tensor_scalar_mul(dst[:, t, :], dst[:, t, :], gain_t[:, b, t:t + 1])
+            else:
+                nc.scalar.mul(dst[:, t, :], dst[:, t, :], gain_t[:, b, t:t + 1])
 
-        vc = [gather_words(table_a0, idx, "vc0"), gather_words(table_a1, idx, "vc1")]
         w1q = {}
+        for a in (1, 0):
+            w1q[a, 0] = quantise_w1(w1_raw[a, 0], a, 0)
+            w1_raw[a, 1] = load_w1(a, 1)
 
-        picked_b = [keep.tile([P, 4, J], F32, name="picked_b%d" % b) for b in range(2)]
+        vc = []
+        gated = [keep.tile([P, 4, J], F32, name="gated0"), None]
+        picked_b = []
         for c in range(8):
             b, t = divmod(c, 4)
             cols = slice(P * c, P * (c + 1))
-            b_row = first_stage([(w2c[:, 2 * P * c:2 * P * (c + 1)].bitcast(FP4X4), w2s[:, cols], v2c, v2s, PLANE_V2)])
-            nc.vector.tensor_copy(picked_b[b][:, t, :], b_row[:].indirect(p2[:]))
-            if c in (3, 5):
-                a = len(w1q)
-                w1q[a, 0] = quantise_w1(w1_raw[a, 0], a, 0)
+            b_row = first_stage([(w2c[:, 2 * P * c:2 * P * (c + 1)].bitcast(FP4X4), w2s[:, cols], v2c, v2s, PLANE_V2)],
+                                "b%d" % c, SLOT[c] + (0 if c in (0, 2) else 64))
+            if c == 0:
+                picked_b.append(keep.tile([P, J], F32, name="picked_b%d" % c))
+            else:
+                picked_b.append(placed([P, J], F32, "picked_b%d" % c, A0 + 2048 * (c - 1) if c < 3 else A1 + 2048 * (c - 3)))
+            nc.vector.tensor_copy(picked_b[c][:], b_row[:].indirect(p2[:]))
+            probe(8 + c, picked_b[c][:, 0:1])
+            if c in (0, 2):
+                vc.append(gather_words((table_a0, table_a1)[len(vc)], idx, placed([P, S], U32, "vc%d" % c, SLOT[c] + 64 - 4096)))
+            if c in (4, 5, 6, 7):
+                finish_gate((4, 5, 6, 7).index(c), gated[0])
 
-        def make_z(b, a_rows, lo, hi):
+        w4_raw = placed([P, 2, 4, N], F32, "w4raw", W4R)
+        nc.sync.dma_start(w4_raw[:], w4.rearrange("(a p j) n -> p a j n", a=2, j=4))
+        def new_sq(b, lo, hi):
+            return ring.tile([P, 4, hi - lo], F32, name="sq%d_%d" % (b, lo), tag="sq%d" % b, bufs=1)
+
+        def diff(sq, b, t, a_row, lo, hi):
+            nc.vector.tensor_tensor(sq[:, t, :], a_row[:].indirect(p1[:, lo // 16:hi // 16]), picked_b[4 * b + t][:, lo:hi], ALU.subtract)
+            probe(16 + 4 * b + t + (8 if lo else 0), sq[:, t, 0:1])
+
+        def square(sq, t):
+            nc.scalar.activation(sq[:, t, :], sq[:, t, :], ACT.Square)
+
+        def make_z(b, sq, lo, hi):
             w = hi - lo
-            sq = keep.tile([P, 4, w], F32, name="sq%d_%d" % (b, lo))
-            for t in range(4):
-                nc.vector.tensor_tensor(sq[:, t, :], a_rows[t][:].indirect(p1[:, lo // 16:hi // 16]),
-                                        picked_b[b][:, t, lo:hi], ALU.subtract)
-                nc.scalar.activation(sq[:, t, :], sq[:, t, :], ACT.Square)
             zbf = keep.tile([P, 4 * w], BF16, name="zbf%d_%d" % (b, lo), align_bytes=64)
             nc.vector.tensor_tensor(zbf[:].rearrange("p (c i t) -> p c t i", i=4, t=4),
                                     sq[:].rearrange("p t (c i) -> p c t i", i=4),
-                                    gate[b][:, :, lo:hi].rearrange("p t (c i) -> p c t i", i=4), ALU.mult)
+                                    gated[b][:, :, lo:hi].rearrange("p t (c i) -> p c t i", i=4), ALU.mult)
             zc = keep.tile([P, w], U32, name="zc%d_%d" % (b, lo), align_bytes=64)
             zs = keep.tile([P, w], U8, name="zs%d_%d" % (b, lo), align_bytes=64)
-            nc.vector.quantize_mx(out=zc[:].bitcast(FP8X4), scales=zs[:], in_=zbf[:])
+            for q0, q1 in ((0, 256), (256, w)) if w == 384 else ((0, w),):
+                nc.vector.quantize_mx(out=zc[:, q0:q1].bitcast(FP8X4), scales=zs[:, q0:q1], in_=zbf[:, 4 * q0:4 * q1])
             return zc, zs
 
-        def a_rows_of(b):
-            rows = []
-            for t in range(4):
-                cols = slice(P * t, P * (t + 1))
-                rows.append(first_stage([
-                    (w1q[a, b][0][:, cols].bitcast(FP8X4), w1q[a, b][1][:, cols], vc[a], vs, PLANE_V + 4 * a)
-                    for a in range(2)]))
-            return rows
+        def a_row(c):
+            b, t = divmod(c, 4)
+            cols = slice(P * t, P * (t + 1))
+            return first_stage([
+                (w1q[a, b][0][:, cols].bitcast(FP8X4), w1q[a, b][1][:, cols], vc[a], vs, PLANE_V + 4 * a) for a in range(2)],
+                "a%d" % c, SLOT[c] + 64)
 
-        rows0 = a_rows_of(0)
         for a in range(2):
             w1q[a, 1] = quantise_w1(w1_raw[a, 1], a, 1)
-        finish_gate(0)
-        rows1 = a_rows_of(1)
-        z0 = make_z(0, rows0, 0, J)
-        finish_gate(1)
-        w4c = keep.tile([P, 2 * N], U32, name="w4c", align_bytes=64)
-        w4s = keep.tile([P, 2 * N], U8, name="w4s", align_bytes=64)
+
+        rows = []
+        sq0 = new_sq(0, 0, J)
+        sq1 = new_sq(1, *LAST_CHUNKS[0])
+        for c in range(8):
+            rows.append(a_row(c))
+            if c < 4:
+                diff(sq0, 0, c, rows[c], 0, J)
+            else:
+                diff(sq1, 1, c - 4, rows[c], *LAST_CHUNKS[0])
+            if 3 <= c < 7:
+                square(sq0, c - 3)
+
+        gated[1] = placed([P, 4, J], F32, "gated1", SLOT[0] + 64)
+        for c in range(4, 8):
+            finish_gate(c, gated[1])
+        z0 = make_z(0, sq0, 0, J)
+
+        for t in range(4):
+            square(sq1, t)
         for a in range(2):
-            raw = placed([P, 4, N], F32, "w4raw%d" % a, RAW + 8 * a)
-            nc.sync.dma_start(raw[:], w4[KP * a:KP * (a + 1), :].rearrange("(p j) n -> p j n", j=4))
-            w4bf = ring.tile([P, 4 * N], BF16, name="w4bf", tag="bf", bufs=2, align_bytes=64)
-            cast(w4bf[:].rearrange("p (c i j) -> p c j i", i=4, j=4), raw[:].rearrange("p j (c i) -> p c j i", i=4))
-            for lo, hi in ((0, 256), (256, N)):
-                nc.vector.quantize_mx(out=w4c[:, N * a + lo:N * a + hi].bitcast(FP8X4), scales=w4s[:, N * a + lo:N * a + hi],
-                                      in_=w4bf[:, 4 * lo:4 * hi])
+            quantise_w4(a, nc.scalar.copy)
 
         out_v = out.rearrange("(i p) j -> p i j", p=P)
         for lo, hi in LAST_CHUNKS:
-            z1 = make_z(1, rows1, lo, hi)
+            if lo:
+                sq1 = new_sq(1, lo, hi)
+                for t in range(4):
+                    diff(sq1, 1, t, rows[4 + t], lo, hi)
+                    square(sq1, t)
+            z1 = make_z(1, sq1, lo, hi)
             for j0 in range(lo, hi, P):
                 zp = [(z0[0][:, j0:j0 + P], z0[1][:, j0:j0 + P]),
                       (z1[0][:, j0 - lo:j0 - lo + P], z1[1][:, j0 - lo:j0 - lo + P])]
@@ -242,6 +319,6 @@ def tile_list_laundry_batch_scores_kernel(
                                             rhs=zp[b][0].bitcast(FP8X4), rhs_scale=zp[b][1], start=(b == 0), stop=(b == 1))
                 bounded = ring.tile([P, 3, P], F32, name="bounded", tag="bounded", bufs=2)
                 nc.scalar.activation(bounded[:], y4[:], ACT.Tanh)
-                res = ring.tile([P, 3, P], F32, name="res", tag="res", bufs=3)
+                res = ring.tile([P, 3, P], F32, name="res", tag="res", bufs=4)
                 nc.vector.tensor_tensor(res[:], y5[:], bounded[:], ALU.add)
                 nc.sync.dma_start(out_v[:, :, j0:j0 + P], res[:])

@@ -24,19 +24,17 @@ N = 384
 KP = 512
 PLANE_V2, PLANE_V3, PLANE_V = 0, 4, 8
 PLANE_W2, PLANE_W3 = 0, 4
-V3C = 0
-V3 = V3C + 4096 - 64
-W1_AT = (V3 + 4096 - 64, V3 + 4096 - 64 + 8192)
-A1 = W1_AT[1] + 8192
+A1 = 0
 T2 = A1 + 16384 - 64
-T3 = T2 + 16384 - 64
-V2S = T3 + 16384 - 64
-W4R = V2S + 1024 - 64
-V2 = W4R + 12288
-D0 = V2 + 4096 - 64
-VP = D0 + 2048 - 64
-A0 = VP + 64
-ROWS = A0 + 16384
+V2 = T2 + 16384 - 64
+W1_AT = (V2 + 4096 - 64, V2 + 4096 - 64 + 8192)
+V3C = W1_AT[1] + 8192
+W3C = V3C + 4096 + 64
+T3 = W3C + 4096
+A0 = T3 + 16384 - 64
+W4R = A0 + 16384 - 64
+D1 = W4R + 12288
+ROWS = D1 + 8192 + 1024
 PAD = (4096, 0, 4096, 4096, 0, 0, 0, 0)
 SLOT = [ROWS + sum(PAD[:i + 1]) + 4160 * i for i in range(8)]
 LAST_CHUNKS = ((0, 384), (384, 512))
@@ -119,11 +117,11 @@ def tile_list_laundry_batch_scores_kernel(
             nc.scalar.copy(dst, src)
 
         def quantise_w1(raw, a, b):
-            bf = ring.tile([P, 2048], BF16, name="bf", tag="bf", bufs=2, align_bytes=64)
+            bf = placed([P, 2048], BF16, "bf%d%d" % (a, b), (V3C + 64, W3C)[a])
             cast(bf[:].rearrange("p (t m j) -> p m j t", t=4, j=4), raw[:].rearrange("p j (m t) -> p m j t", t=4))
-            at = (T2 + 64 + 3072 + 8192, A1 + 10240)[b] + 2560 * a
+            at = (T2 + 64 + 4096, A1 + 10240)[b] + 2560 * a
             codes = placed([P, 512], U32, "w1c%d%d" % (a, b), at)
-            scales = placed([P, 512], U8, "w1s%d%d" % (a, b), at + 2048)
+            scales = placed([P, 512], U8, "w1s%d%d" % (a, b), at + 2048 if b else D1 + 8192 + 512 * a)
             nc.vector.quantize_mx(out=codes[:].bitcast(FP8X4), scales=scales[:], in_=bf[:])
             return codes, scales
 
@@ -133,51 +131,64 @@ def tile_list_laundry_batch_scores_kernel(
             if i in ():
                 nc.gpsimd.tensor_copy(clock[:, i:i + 1], ap)
 
-        v3_plane = zeroed(placed([P, T], U8, "v3_plane", V3), nc.vector)
+        def scale_window(t, scales):
+            first = P - 16 * scales.shape[0]
+            nc.vector.memset(t[0:first, :].bitcast(I32), 0)
+            nc.sync.dma_start(t[first:P, :].bitcast(I32), scales.rearrange("a q t -> (a q) t").bitcast(I32))
+            return t
+
+        def move_scale_rows(plane, first_row, picked, passes):
+            for a in range(passes):
+                for q in range(4):
+                    src = P - 16 * (passes - a) + 4 * q
+                    dst = 32 * q + first_row + 4 * a
+                    nc.sync.dma_start(plane[dst:dst + 4, :].bitcast(I32), picked[src:src + 4, :].bitcast(I32))
+            return plane
+
         w3_plane = zeroed(keep.tile([P, H], U8, name="w3_plane", align_bytes=64), nc.gpsimd)
-        v2_plane = zeroed(placed([P, T], U8, "v2_plane", V2), nc.vector)
-        v_plane = zeroed(placed([P, T], U8, "v_plane", VP), nc.vector)
-        w2_plane = zeroed(keep.tile([P, H], U8, name="w2_plane", align_bytes=64), nc.vector)
-        warm = keep.tile([P, 8], F32, name="warm")
-        nc.vector.memset(warm[:], 0.0)
-        nc.scalar.activation(warm[:, 1:2], warm[:, 0:1], ACT.Sigmoid)
         idx3 = load_list(offs3, "idx3")
-        idx = load_list(offs, "idx")
+        v3_win = scale_window(placed([P, T], U8, "v3_win", V3C), tab3_scales)
         idx2 = load_list(offs2, "idx2")
+        v2_win = scale_window(placed([P, T], U8, "v2_win", V2), tab2_scales)
+        idx = load_list(offs, "idx")
         p3 = load_list(pos3, "p3")
-        p2 = load_list(pos2, "p2")
-        p1 = load_list(pos1, "p1")
         w3_raw = placed([P, H], I32, "w3_raw", W1_AT[1])
         nc.sync.dma_start(w3_raw[:], w3_words[0].rearrange("p c i -> p (c i)").bitcast(I32))
         table3 = load_table_words(tab3_words, 0, "table3", T3)
-        w4_raw = {}
-
-        load_scale_rows([nc.scalar] * 4, v3_plane, PLANE_V3, tab3_scales)
-        load_scale_rows([nc.gpsimd] * 2 + [nc.scalar] * (4 - 2), w3_plane, 0, w3_scales)
-        load_scale_rows([nc.gpsimd] * 4, v2_plane, PLANE_V2, tab2_scales)
-        load_scale_rows([nc.sync] * 4, v_plane, PLANE_V, tab_scales)
-        load_scale_rows([nc.sync] * 4, w2_plane, 0, w2_scales)
+        p2 = load_list(pos2, "p2")
+        p1 = load_list(pos1, "p1")
+        load_scale_rows([nc.gpsimd] * 4, w3_plane, 0, w3_scales)
+        w2_plane = zeroed(placed([P, H], U8, "w2_plane", D1 + 8192 - 64), nc.vector)
+        load_scale_rows([nc.gpsimd] * 4, w2_plane, 0, w2_scales)
+        v2s = zeroed(keep.tile([P, S], U8, name="v2s", align_bytes=64), nc.vector)
+        v3s = zeroed(keep.tile([P, S], U8, name="v3s", align_bytes=64), nc.vector)
+        warm = keep.tile([P, 8], F32, name="warm")
+        nc.vector.memset(warm[:], 0.0)
+        nc.scalar.activation(warm[:, 1:2], warm[:, 0:1], ACT.Sigmoid)
 
         def deal(src, dtype, dst):
             nc.vector.tensor_copy(dst[:].bitcast(dtype).rearrange("p (b t m) -> p b t m", b=2, t=4),
                                   src[:].bitcast(dtype).rearrange("p (b m t) -> p b t m", b=2, t=4))
             return dst
 
-        w3c = keep.tile([P, H], I32, name="w3c", align_bytes=64)
-        nc.vector.tensor_copy(w3c[:].rearrange("p (b t m) -> p b m t", b=2, t=4), w3_raw[:].rearrange("p (b m t) -> p b m t", b=2, t=4))
-        w1_raw = {}
-        w1_raw[1, 0] = load_w1(1, 0)
-        v3s = gather_scales(v3_plane, idx3, keep.tile([P, S], U8, name="v3s", align_bytes=64))
-        w1_raw[0, 0] = load_w1(0, 0)
-        w3s = deal(w3_plane, U8, keep.tile([P, H], U8, name="w3s", align_bytes=64))
-        v3c = placed([P, S], U32, "v3c", V3C)
-        for h in range(2):
-            nc.vector.tensor_copy(v3c[:, 512 * h:512 * (h + 1)], table3[:].bitcast(U32).indirect(idx3[:, 32 * h:32 * (h + 1)]))
+        def picked_scales(window, lst, name):
+            return gather_scales(window, lst, keep.tile([P, S], U8, name=name, align_bytes=64))
+
+        move_scale_rows(v3s, PLANE_V3, picked_scales(v3_win, idx3, "v3g"), 1)
+        v2g = picked_scales(v2_win, idx2, "v2g")
         table2 = load_table_words(tab2_words, 0, "table2", T2)
-        w2_raw = placed([P, 2 * H], U8, "w2_raw", T3 + 64)
+        w2_raw = placed([P, 2 * H], U8, "w2_raw", V2 + 64)
         nc.sync.dma_start(w2_raw[:].bitcast(I32), w2_words[0].bitcast(I32))
-        v2s = gather_scales(v2_plane, idx2, placed([P, S], U8, "v2s", V2S))
-        vs = gather_scales(v_plane, idx, placed([P, S], U8, "vs", T3 + 4096))
+        w1_raw = {}
+        w1_raw[0, 0] = load_w1(0, 0)
+        w3c = placed([P, H], I32, "w3c", W3C)
+        nc.vector.tensor_copy(w3c[:].rearrange("p (b t m) -> p b m t", b=2, t=4), w3_raw[:].rearrange("p (b m t) -> p b m t", b=2, t=4))
+        w1_raw[1, 0] = load_w1(1, 0)
+        move_scale_rows(v2s, PLANE_V2, v2g, 1)
+        v3c = gather_words(table3, idx3, placed([P, S], U32, "v3c", V3C))
+        w3s = deal(w3_plane, U8, placed([P, H], U8, "w3s", T3 + 4096))
+        v_plane = zeroed(placed([P, T], U8, "v_plane", T3), nc.vector)
+        load_scale_rows([nc.sync] * 4, v_plane, PLANE_V, tab_scales)
         table_a0 = load_table_words(tab_words, 0, "table_a0", A0)
         gain_t = placed([P, 2, 4], F32, "gain_t", T3 + 5120)
         nc.sync.dma_start(gain_t[:], gain.rearrange("(b p t) -> p b t", b=2, t=4))
@@ -188,33 +199,31 @@ def tile_list_laundry_batch_scores_kernel(
             nc.sync.dma_start(w5s[32 * q:32 * q + 4, :].rearrange("r (a n) -> r a n", a=2).bitcast(I32),
                               w5_scales[:, 4 * q:4 * q + 4, :].rearrange("a r n -> r a n").bitcast(I32))
 
-        picked_d = []
+        picked_d = [keep.tile([P, 4, J], F32, name="picked_d0")]
         for c in range(8):
             if c == 4:
                 v2c = gather_words(table2, idx2, placed([P, S], U32, "v2c", SLOT[3] + 64 - 4096))
                 table_a1 = load_table_words(tab_words, 1, "table_a1", A1)
                 w2c = deal(w2_raw, U16, placed([P, 2 * H], U8, "w2c", T2 + 64))
                 w2s = deal(w2_plane, U8, placed([P, H], U8, "w2s", T2 + 64 + 2048))
+                vs = gather_scales(v_plane, idx, placed([P, S], U8, "vs", T2 + 64 + 3072))
+                picked_d.append(placed([P, 4, J], F32, "picked_d1", D1))
             b, t = divmod(c, 4)
             cols = slice(P * c, P * (c + 1))
             d_row = first_stage([(w3c[:, cols].bitcast(FP8X4), w3s[:, cols], v3c, v3s, PLANE_V3)], "d%d" % c, SLOT[c])
-            if c in (0, 4, 5, 6, 7):
-                picked_d.append(placed([P, J], F32, "picked_d%d" % c, D0 if c == 0 else T2 + 64 + 3072 + 2048 * (c - 4)))
-            else:
-                picked_d.append(keep.tile([P, J], F32, name="picked_d%d" % c))
-            nc.vector.tensor_copy(picked_d[c][:], d_row[:].indirect(p3[:]))
-            probe(c, picked_d[c][:, 0:1])
+            nc.vector.tensor_copy(picked_d[b][:, t, :], d_row[:].indirect(p3[:]))
+            probe(c, picked_d[b][:, t, 0:1])
 
         def finish_gate(c, dst):
             b, t = divmod(c, 4)
-            nc.scalar.activation(dst[:, t, :], picked_d[c][:], ACT.Sigmoid)
+            nc.scalar.activation(dst[:, t, :], picked_d[b][:, t, :], ACT.Sigmoid)
             if c in (4, 5, 6, 7):
                 nc.vector.tensor_scalar_mul(dst[:, t, :], dst[:, t, :], gain_t[:, b, t:t + 1])
             else:
                 nc.scalar.mul(dst[:, t, :], dst[:, t, :], gain_t[:, b, t:t + 1])
 
         w1q = {}
-        for a in (1, 0):
+        for a in range(2):
             w1q[a, 0] = quantise_w1(w1_raw[a, 0], a, 0)
             w1_raw[a, 1] = load_w1(a, 1)
 

from contextlib import ExitStack

import concourse.mybir as mybir

F32 = mybir.dt.float32
BF16 = mybir.dt.bfloat16
I32 = mybir.dt.int32
U32 = mybir.dt.uint32
U16 = mybir.dt.uint16
U8 = mybir.dt.uint8
FP8X4 = mybir.dt.float8_e4m3fn_x4
FP4X4 = mybir.dt.float4_e2m1fn_x4
ACT = mybir.ActivationFunctionType
ALU = mybir.AluOpType

FLOPS = 5100273664

P = 128
T = 4096
S = 1024
J = 512
H = 1024
N = 384
KP = 512
PLANE_V2, PLANE_V3, PLANE_V = 0, 4, 8
PLANE_W2, PLANE_W3 = 0, 4
A1 = 0
T2 = A1 + 16384 - 64
V2 = T2 + 16384 - 64
W1_AT = (V2 + 4096 - 64, V2 + 4096 - 64 + 8192)
V3C = W1_AT[1] + 8192
W3C = V3C + 4096 + 64
T3 = W3C + 4096
A0 = T3 + 16384 - 64
W4R = A0 + 16384 - 64
D1 = W4R + 12288
ROWS = D1 + 8192 + 1024
PAD = (4096, 0, 4096, 4096, 0, 0, 0, 0)
SLOT = [ROWS + sum(PAD[:i + 1]) + 4160 * i for i in range(8)]
LAST_CHUNKS = ((0, 384), (384, 512))


def tile_list_laundry_batch_scores_kernel(
    tc, tab_words, tab_scales, tab2_words, tab2_scales, tab3_words, tab3_scales, offs, offs2, offs3,
    pos1, pos2, pos3, w1, w2_words, w2_scales, w3_words, w3_scales, gain, w4, w5_words, w5_scales, out,
):
    nc = tc.nc
    with ExitStack() as ctx:
        keep = ctx.enter_context(tc.tile_pool(name="keep", bufs=1))
        ring = ctx.enter_context(tc.tile_pool(name="ring", bufs=3))
        shared = ctx.enter_context(tc.tile_pool(name="shared", bufs=1))
        psum = ctx.enter_context(tc.psum_pool(name="psum", bufs=8))

        def load_list(src, name):
            t = keep.tile(list(src.shape), U16, name=name)
            nc.sync.dma_start(t[:], src)
            return t

        def zeroed(t, eng):
            eng.memset(t[:].bitcast(I32), 0)
            return t

        def placed(shape, dtype, name, kib):
            return shared.tile(shape, dtype, name=name, offset=kib, align_bytes=64)

        def load_scale_rows(eng, plane, first_row, scales):
            rows = 4 * scales.shape[0]
            for q in range(4):
                p0 = 32 * q + first_row
                eng[q].dma_start(plane[p0:p0 + rows, :].bitcast(I32), scales[:, 4 * q:4 * q + 4, :].bitcast(I32))

        def load_table_words(words, a, name, kib):
            t = placed([P, T], I32, name, kib)
            nc.sync.dma_start(t[:], words[a].rearrange("p t i -> p (t i)").bitcast(I32))
            return t

        def gather_words(table, lst, g):
            nc.vector.tensor_copy(g[:], table[:].bitcast(U32).indirect(lst[:]))
            return g

        def gather_scales(plane, lst, g):
            nc.vector.tensor_copy(g[:], plane[:].indirect(lst[:]))
            return g

        def first_stage(passes, name, at):
            row = placed([P, S], F32, name, at)
            for h in range(S // 512):
                cols = slice(512 * h, 512 * (h + 1))
                acc = psum.tile([P, 512], F32, name="acc", tag="bank")
                for i, (wc, ws, vc, vs, k) in enumerate(passes):
                    nc.tensor.matmul_mx(out=acc[:], lhsT=wc, lhsT_scale=ws, rhs=vc[:, cols].bitcast(FP8X4),
                                        rhs_scale=vs[k:P, cols], start=(i == 0), stop=(i == len(passes) - 1))
                nc.scalar.copy(row[:, cols], acc[:])
            return row

        def load_w1(a, b):
            raw = placed([P, 4, 512], F32, "w1raw%d%d" % (a, b), W1_AT[a])
            nc.sync.dma_start(raw[:], w1[KP * a:KP * (a + 1), 512 * b:512 * (b + 1)].rearrange("(p j) c -> p j c", j=4))
            return raw

        def load_w4(a, raw):
            nc.sync.dma_start(raw[:], w4[KP * a:KP * (a + 1), :].rearrange("(p j) n -> p j n", j=4))
            return raw

        w4c = keep.tile([P, 2 * N], U32, name="w4c", align_bytes=64)
        w4s = keep.tile([P, 2 * N], U8, name="w4s", align_bytes=64)

        def quantise_w4(a, cast):
            raw = w4_raw[:, a]
            w4bf = placed([P, 4 * N], BF16, "w4bf%d" % a, SLOT[2 + a] + 64)
            cast(w4bf[:].rearrange("p (c i j) -> p c j i", i=4, j=4), raw.rearrange("p j (c i) -> p c j i", i=4))
            for lo, hi in ((0, 256), (256, N)):
                nc.vector.quantize_mx(out=w4c[:, N * a + lo:N * a + hi].bitcast(FP8X4), scales=w4s[:, N * a + lo:N * a + hi],
                                      in_=w4bf[:, 4 * lo:4 * hi])

        def cast(dst, src):
            nc.scalar.copy(dst, src)

        def quantise_w1(raw, a, b):
            bf = placed([P, 2048], BF16, "bf%d%d" % (a, b), (V3C + 64, W3C)[a])
            cast(bf[:].rearrange("p (t m j) -> p m j t", t=4, j=4), raw[:].rearrange("p j (m t) -> p m j t", t=4))
            at = (T2 + 64 + 4096, A1 + 10240)[b] + 2560 * a
            codes = placed([P, 512], U32, "w1c%d%d" % (a, b), at)
            scales = placed([P, 512], U8, "w1s%d%d" % (a, b), at + 2048 if b else D1 + 8192 + 512 * a)
            nc.vector.quantize_mx(out=codes[:].bitcast(FP8X4), scales=scales[:], in_=bf[:])
            return codes, scales

        clock = keep.tile([P, 32], F32, name="clock")

        def probe(i, ap):
            if i in ():
                nc.gpsimd.tensor_copy(clock[:, i:i + 1], ap)

        def scale_window(t, scales):
            first = P - 16 * scales.shape[0]
            nc.vector.memset(t[0:first, :].bitcast(I32), 0)
            nc.sync.dma_start(t[first:P, :].bitcast(I32), scales.rearrange("a q t -> (a q) t").bitcast(I32))
            return t

        def move_scale_rows(plane, first_row, picked, passes):
            for a in range(passes):
                for q in range(4):
                    src = P - 16 * (passes - a) + 4 * q
                    dst = 32 * q + first_row + 4 * a
                    nc.sync.dma_start(plane[dst:dst + 4, :].bitcast(I32), picked[src:src + 4, :].bitcast(I32))
            return plane

        w3_plane = zeroed(keep.tile([P, H], U8, name="w3_plane", align_bytes=64), nc.gpsimd)
        idx3 = load_list(offs3, "idx3")
        v3_win = scale_window(placed([P, T], U8, "v3_win", V3C), tab3_scales)
        idx2 = load_list(offs2, "idx2")
        v2_win = scale_window(placed([P, T], U8, "v2_win", V2), tab2_scales)
        idx = load_list(offs, "idx")
        p3 = load_list(pos3, "p3")
        w3_raw = placed([P, H], I32, "w3_raw", W1_AT[1])
        nc.sync.dma_start(w3_raw[:], w3_words[0].rearrange("p c i -> p (c i)").bitcast(I32))
        table3 = load_table_words(tab3_words, 0, "table3", T3)
        p2 = load_list(pos2, "p2")
        p1 = load_list(pos1, "p1")
        load_scale_rows([nc.gpsimd] * 4, w3_plane, 0, w3_scales)
        w2_plane = zeroed(placed([P, H], U8, "w2_plane", D1 + 8192 - 64), nc.vector)
        load_scale_rows([nc.gpsimd] * 4, w2_plane, 0, w2_scales)
        v2s = zeroed(keep.tile([P, S], U8, name="v2s", align_bytes=64), nc.vector)
        v3s = zeroed(keep.tile([P, S], U8, name="v3s", align_bytes=64), nc.vector)
        warm = keep.tile([P, 8], F32, name="warm")
        nc.vector.memset(warm[:], 0.0)
        nc.scalar.activation(warm[:, 1:2], warm[:, 0:1], ACT.Sigmoid)

        def deal(src, dtype, dst):
            nc.vector.tensor_copy(dst[:].bitcast(dtype).rearrange("p (b t m) -> p b t m", b=2, t=4),
                                  src[:].bitcast(dtype).rearrange("p (b m t) -> p b t m", b=2, t=4))
            return dst

        def picked_scales(window, lst, name):
            return gather_scales(window, lst, keep.tile([P, S], U8, name=name, align_bytes=64))

        move_scale_rows(v3s, PLANE_V3, picked_scales(v3_win, idx3, "v3g"), 1)
        v2g = picked_scales(v2_win, idx2, "v2g")
        table2 = load_table_words(tab2_words, 0, "table2", T2)
        w2_raw = placed([P, 2 * H], U8, "w2_raw", V2 + 64)
        nc.sync.dma_start(w2_raw[:].bitcast(I32), w2_words[0].bitcast(I32))
        w1_raw = {}
        w1_raw[0, 0] = load_w1(0, 0)
        w3c = placed([P, H], I32, "w3c", W3C)
        nc.vector.tensor_copy(w3c[:].rearrange("p (b t m) -> p b m t", b=2, t=4), w3_raw[:].rearrange("p (b m t) -> p b m t", b=2, t=4))
        w1_raw[1, 0] = load_w1(1, 0)
        move_scale_rows(v2s, PLANE_V2, v2g, 1)
        v3c = gather_words(table3, idx3, placed([P, S], U32, "v3c", V3C))
        w3s = deal(w3_plane, U8, placed([P, H], U8, "w3s", T3 + 4096))
        v_plane = zeroed(placed([P, T], U8, "v_plane", T3), nc.vector)
        load_scale_rows([nc.sync] * 4, v_plane, PLANE_V, tab_scales)
        table_a0 = load_table_words(tab_words, 0, "table_a0", A0)
        gain_t = placed([P, 2, 4], F32, "gain_t", T3 + 5120)
        nc.sync.dma_start(gain_t[:], gain.rearrange("(b p t) -> p b t", b=2, t=4))
        w5c = placed([P, 2, 2 * N], U8, "w5c", T3 + 5184)
        nc.sync.dma_start(w5c[:].bitcast(I32), w5_words.rearrange("a p c -> p a c").bitcast(I32))
        w5s = zeroed(placed([P, 2 * N], U8, "w5s", T3 + 6720), nc.vector)
        for q in range(4):
            nc.sync.dma_start(w5s[32 * q:32 * q + 4, :].rearrange("r (a n) -> r a n", a=2).bitcast(I32),
                              w5_scales[:, 4 * q:4 * q + 4, :].rearrange("a r n -> r a n").bitcast(I32))

        picked_d = [keep.tile([P, 4, J], F32, name="picked_d0")]
        for c in range(8):
            if c == 4:
                v2c = gather_words(table2, idx2, placed([P, S], U32, "v2c", SLOT[3] + 64 - 4096))
                table_a1 = load_table_words(tab_words, 1, "table_a1", A1)
                w2c = deal(w2_raw, U16, placed([P, 2 * H], U8, "w2c", T2 + 64))
                w2s = deal(w2_plane, U8, placed([P, H], U8, "w2s", T2 + 64 + 2048))
                vs = gather_scales(v_plane, idx, placed([P, S], U8, "vs", T2 + 64 + 3072))
                picked_d.append(placed([P, 4, J], F32, "picked_d1", D1))
            b, t = divmod(c, 4)
            cols = slice(P * c, P * (c + 1))
            d_row = first_stage([(w3c[:, cols].bitcast(FP8X4), w3s[:, cols], v3c, v3s, PLANE_V3)], "d%d" % c, SLOT[c])
            nc.vector.tensor_copy(picked_d[b][:, t, :], d_row[:].indirect(p3[:]))
            probe(c, picked_d[b][:, t, 0:1])

        def finish_gate(c, dst):
            b, t = divmod(c, 4)
            nc.scalar.activation(dst[:, t, :], picked_d[b][:, t, :], ACT.Sigmoid)
            if c in (4, 5, 6, 7):
                nc.vector.tensor_scalar_mul(dst[:, t, :], dst[:, t, :], gain_t[:, b, t:t + 1])
            else:
                nc.scalar.mul(dst[:, t, :], dst[:, t, :], gain_t[:, b, t:t + 1])

        w1q = {}
        for a in range(2):
            w1q[a, 0] = quantise_w1(w1_raw[a, 0], a, 0)
            w1_raw[a, 1] = load_w1(a, 1)

        vc = []
        gated = [keep.tile([P, 4, J], F32, name="gated0"), None]
        picked_b = []
        for c in range(8):
            b, t = divmod(c, 4)
            cols = slice(P * c, P * (c + 1))
            b_row = first_stage([(w2c[:, 2 * P * c:2 * P * (c + 1)].bitcast(FP4X4), w2s[:, cols], v2c, v2s, PLANE_V2)],
                                "b%d" % c, SLOT[c] + (0 if c in (0, 2) else 64))
            if c == 0:
                picked_b.append(keep.tile([P, J], F32, name="picked_b%d" % c))
            else:
                picked_b.append(placed([P, J], F32, "picked_b%d" % c, A0 + 2048 * (c - 1) if c < 3 else A1 + 2048 * (c - 3)))
            nc.vector.tensor_copy(picked_b[c][:], b_row[:].indirect(p2[:]))
            probe(8 + c, picked_b[c][:, 0:1])
            if c in (0, 2):
                vc.append(gather_words((table_a0, table_a1)[len(vc)], idx, placed([P, S], U32, "vc%d" % c, SLOT[c] + 64 - 4096)))
            if c in (4, 5, 6, 7):
                finish_gate((4, 5, 6, 7).index(c), gated[0])

        w4_raw = placed([P, 2, 4, N], F32, "w4raw", W4R)
        nc.sync.dma_start(w4_raw[:], w4.rearrange("(a p j) n -> p a j n", a=2, j=4))
        def new_sq(b, lo, hi):
            return ring.tile([P, 4, hi - lo], F32, name="sq%d_%d" % (b, lo), tag="sq%d" % b, bufs=1)

        def diff(sq, b, t, a_row, lo, hi):
            nc.vector.tensor_tensor(sq[:, t, :], a_row[:].indirect(p1[:, lo // 16:hi // 16]), picked_b[4 * b + t][:, lo:hi], ALU.subtract)
            probe(16 + 4 * b + t + (8 if lo else 0), sq[:, t, 0:1])

        def square(sq, t):
            nc.scalar.activation(sq[:, t, :], sq[:, t, :], ACT.Square)

        def make_z(b, sq, lo, hi):
            w = hi - lo
            zbf = keep.tile([P, 4 * w], BF16, name="zbf%d_%d" % (b, lo), align_bytes=64)
            nc.vector.tensor_tensor(zbf[:].rearrange("p (c i t) -> p c t i", i=4, t=4),
                                    sq[:].rearrange("p t (c i) -> p c t i", i=4),
                                    gated[b][:, :, lo:hi].rearrange("p t (c i) -> p c t i", i=4), ALU.mult)
            zc = keep.tile([P, w], U32, name="zc%d_%d" % (b, lo), align_bytes=64)
            zs = keep.tile([P, w], U8, name="zs%d_%d" % (b, lo), align_bytes=64)
            for q0, q1 in ((0, 256), (256, w)) if w == 384 else ((0, w),):
                nc.vector.quantize_mx(out=zc[:, q0:q1].bitcast(FP8X4), scales=zs[:, q0:q1], in_=zbf[:, 4 * q0:4 * q1])
            return zc, zs

        def a_row(c):
            b, t = divmod(c, 4)
            cols = slice(P * t, P * (t + 1))
            return first_stage([
                (w1q[a, b][0][:, cols].bitcast(FP8X4), w1q[a, b][1][:, cols], vc[a], vs, PLANE_V + 4 * a) for a in range(2)],
                "a%d" % c, SLOT[c] + 64)

        for a in range(2):
            w1q[a, 1] = quantise_w1(w1_raw[a, 1], a, 1)

        rows = []
        sq0 = new_sq(0, 0, J)
        sq1 = new_sq(1, *LAST_CHUNKS[0])
        for c in range(8):
            rows.append(a_row(c))
            if c < 4:
                diff(sq0, 0, c, rows[c], 0, J)
            else:
                diff(sq1, 1, c - 4, rows[c], *LAST_CHUNKS[0])
            if 3 <= c < 7:
                square(sq0, c - 3)

        gated[1] = placed([P, 4, J], F32, "gated1", SLOT[0] + 64)
        for c in range(4, 8):
            finish_gate(c, gated[1])
        z0 = make_z(0, sq0, 0, J)

        for t in range(4):
            square(sq1, t)
        for a in range(2):
            quantise_w4(a, nc.scalar.copy)

        out_v = out.rearrange("(i p) j -> p i j", p=P)
        for lo, hi in LAST_CHUNKS:
            if lo:
                sq1 = new_sq(1, lo, hi)
                for t in range(4):
                    diff(sq1, 1, t, rows[4 + t], lo, hi)
                    square(sq1, t)
            z1 = make_z(1, sq1, lo, hi)
            for j0 in range(lo, hi, P):
                zp = [(z0[0][:, j0:j0 + P], z0[1][:, j0:j0 + P]),
                      (z1[0][:, j0 - lo:j0 - lo + P], z1[1][:, j0 - lo:j0 - lo + P])]
                y4 = psum.tile([P, 3, P], F32, name="y4", tag="bank")
                y5 = psum.tile([P, 3, P], F32, name="y5", tag="bank")
                for i in range(3):
                    for b in range(2):
                        n0 = N * b + P * i
                        nc.tensor.matmul_mx(out=y4[:, i, :], lhsT=w4c[:, n0:n0 + P].bitcast(FP8X4), lhsT_scale=w4s[:, n0:n0 + P],
                                            rhs=zp[b][0].bitcast(FP8X4), rhs_scale=zp[b][1], start=(b == 0), stop=(b == 1))
                for i in range(3):
                    for b in range(2):
                        n0 = N * b + P * i
                        nc.tensor.matmul_mx(out=y5[:, i, :], lhsT=w5c[:, b, 2 * P * i:2 * P * (i + 1)].bitcast(FP4X4),
                                            lhsT_scale=w5s[:, n0:n0 + P],
                                            rhs=zp[b][0].bitcast(FP8X4), rhs_scale=zp[b][1], start=(b == 0), stop=(b == 1))
                bounded = ring.tile([P, 3, P], F32, name="bounded", tag="bounded", bufs=2)
                nc.scalar.activation(bounded[:], y4[:], ACT.Tanh)
                res = ring.tile([P, 3, P], F32, name="res", tag="res", bufs=4)
                nc.vector.tensor_tensor(res[:], y5[:], bounded[:], ALU.add)
                nc.sync.dma_start(out_v[:, :, j0:j0 + P], res[:])
